import numpy as np
import ml_dtypes


def mxq(x, axis, fmt="e4m3"):
    dtype, down = {"e4m3": (ml_dtypes.float8_e4m3fn, 7), "e5m2": (ml_dtypes.float8_e5m2, 14)}[fmt]
    v = np.moveaxis(np.asarray(x, np.float32).astype(ml_dtypes.bfloat16).astype(np.float64), axis, -1)
    blocks = v.reshape(v.shape[:-1] + (-1, 32))
    amax = np.abs(blocks).max(-1, keepdims=True)
    byte = np.maximum(np.where(amax > 0, np.frexp(amax)[1] - 1 + 127, 0) - down, 1)
    scale = np.exp2(byte - 127.0)
    codes = (blocks / scale).astype(np.float32).astype(dtype).astype(np.float64)
    return np.moveaxis((codes * scale).reshape(v.shape), -1, axis)


WIDE = False


def mx_kscale(k):
    if not WIDE:
        return np.ones(k)
    levels = np.array([30, -30])
    if k % 512:
        return np.exp2(np.random.permutation(np.resize(levels, k // 32))).repeat(32)
    a = np.empty((k // 512, 16))
    for p in range(k // 512):
        a[p, :8] = np.random.permutation(np.resize(levels, 8))
        for g in range(8):
            far = levels[np.abs(levels - a[p, g]) >= 10]
            a[p, g + 8] = far[np.random.randint(len(far))]
    return np.exp2(a.ravel()).repeat(32)


def f64(x):
    return np.asarray(x).astype(np.float64)


def striped(idx):
    return np.tile(np.asarray(idx).reshape(-1, 16).T, (8, 1)).astype(np.uint16)


def unstriped(offs):
    return offs[:16].T.reshape(-1).astype(np.int64)


E2M1 = np.array([0.0, 0.5, 1.0, 1.5, 2.0, 3.0, 4.0, 6.0, -0.0, -0.5, -1.0, -1.5, -2.0, -3.0, -4.0, -6.0])


def pack_weight(w, fmt):
    k, n = w.shape
    w = f64(np.asarray(w, np.float32).astype(ml_dtypes.bfloat16)).reshape(k // 32, 32, n)
    amax = np.abs(w).max(1)
    if fmt in ("e4m3", "e5m2"):
        byte = np.frexp(amax)[1] - 1 + 127 - (7 if fmt == "e4m3" else 14)
    else:
        mant, ex = np.frexp(amax / 6.0)
        byte = np.where(mant > 0.5, ex, ex - 1) + 127
    byte = np.clip(np.where(amax > 0, byte, 1), 1, 254)
    scaled = (w * np.exp2(127.0 - byte)[:, None, :]).reshape(k, n).astype(np.float32)
    by_word = np.ascontiguousarray(scaled.reshape(k // 512, 128, 4, n).transpose(0, 1, 3, 2))
    if fmt in ("e4m3", "e5m2"):
        words = by_word.astype(ml_dtypes.float8_e4m3fn if fmt == "e4m3" else ml_dtypes.float8_e5m2).view(np.uint8)
    else:
        c = by_word.astype(ml_dtypes.float4_e2m1fn).view(np.uint8) & 0xF
        words = (c[..., 0::2] | (c[..., 1::2] << 4)).reshape(k // 512, 128, 2 * n)
    return np.ascontiguousarray(words), np.ascontiguousarray(byte.astype(np.uint8).reshape(k // 512, 16, n))


def unpack_weight(words, scales, fmt):
    g, _, n = scales.shape
    words = np.ascontiguousarray(words).reshape(g, 128, n, -1)
    if fmt in ("e4m3", "e5m2"):
        vals = words.view(ml_dtypes.float8_e4m3fn if fmt == "e4m3" else ml_dtypes.float8_e5m2).astype(np.float64)
    else:
        nib = np.empty((g, 128, n, 4), np.uint8)
        nib[..., 0::2] = words & 0xF
        nib[..., 1::2] = words >> 4
        vals = E2M1[nib]
    vals = vals * np.repeat(np.exp2(scales.astype(np.float64) - 127.0), 8, axis=1)[..., None]
    return vals.transpose(0, 1, 3, 2).reshape(g * 512, n)


def sigmoid(v):
    return 1.0 / (1.0 + np.exp(-v))


def bf(x):
    return np.asarray(x, np.float32).astype(ml_dtypes.bfloat16)


def planes(Y):
    r, m = Y.shape
    b = f64(bf(Y)).reshape(r // 32, 32, m)
    amax = np.abs(b).max(1)
    byte = np.clip(np.where(amax > 0, np.frexp(amax)[1] - 1 + 127 - 7, 1), 1, 254)
    codes = (b * np.exp2(127.0 - byte)[:, None, :]).reshape(r, m).astype(np.float32).astype(ml_dtypes.float8_e4m3fn).view(np.uint8)
    words = codes.reshape(r // 512, 128, 4, m).transpose(0, 1, 3, 2)
    return np.ascontiguousarray(words), np.ascontiguousarray(byte.astype(np.uint8).reshape(r // 512, 16, m))


K, T, J, R, F, Z, N, C = 512, 512, 256, 512, 512, 1024, 512, 512


def setup_inputs():
    n = np.random.standard_normal
    idx = np.random.permutation(T)[:J]
    idx2 = np.random.permutation(Z)[:J]
    idx3 = np.random.permutation(C)[:J]
    fk = mx_kscale(K)
    fr = mx_kscale(R)
    ff = mx_kscale(F)
    xtp = pack_weight(n((K, T)) / fk[:, None], "e5m2")
    wp = pack_weight(n((K, R)) * 1 / np.sqrt(K) * fk[:, None] * fr, "e4m3")
    w2p = pack_weight(n((F, R)) * 1 / np.sqrt(F) * ff[:, None] * fr, "e5m2")
    wbp = pack_weight(n((R, N)) * 1 / np.sqrt(R) / fr[:, None], "e2m1")
    return {
        "xt_words": xtp[0],
        "xt_scales": xtp[1],
        "w_words": wp[0],
        "w_scales": wp[1],
        "xo": (n((F, Z))).astype(np.float32),
        "fl": (np.random.uniform(0.5, 2.0, (F, 1)) / ff[:, None]).astype(np.float32),
        "so": (n((F, J))).astype(np.float32),
        "w2_words": w2p[0],
        "w2_scales": w2p[1],
        "wb_words": wbp[0],
        "wb_scales": wbp[1],
        "tz": (n((N, C))).astype(np.float32),
        "offs": striped(idx),
        "offs2": striped(idx2),
        "offs3": striped(idx3),
    }


def reference(xt_words, xt_scales, w_words, w_scales, xo, fl, so, w2_words, w2_scales, wb_words, wb_scales, tz, offs, offs2, offs3):
    idx = unstriped(offs)
    idx2 = unstriped(offs2)
    idx3 = unstriped(offs3)
    xtu = unpack_weight(xt_words, xt_scales, "e5m2")
    wu = unpack_weight(w_words, w_scales, "e4m3")
    w2u = unpack_weight(w2_words, w2_scales, "e5m2")
    wbu = unpack_weight(wb_words, wb_scales, "e2m1")
    u2 = f64(xo)[:, idx2] * sigmoid(f64(so)) * f64(fl)
    xtidxg = xtu[:, idx]
    u2q = mxq(u2, 0, "e4m3")
    a = wu.T @ xtidxg + w2u.T @ u2q
    hid = np.maximum(a, 0.0)
    hidq = mxq(hid, 0, "e5m2")
    p = wbu.T @ hidq
    y = p * f64(tz)[:, idx3]
    words, scales = planes(y)
    return y, words, scales

@@ -1,0 +1,210 @@
+from contextlib import ExitStack
+
+import concourse.mybir as mybir
+
+F32 = mybir.dt.float32
+BF16 = mybir.dt.bfloat16
+I32 = mybir.dt.int32
+U32 = mybir.dt.uint32
+U16 = mybir.dt.uint16
+U8 = mybir.dt.uint8
+E4M3 = mybir.dt.float8_e4m3fn_x4
+E5M2 = mybir.dt.float8_e5m2_x4
+E2M1 = mybir.dt.float4_e2m1fn_x4
+ACT = mybir.ActivationFunctionType
+ALU = mybir.AluOpType
+
+P = 128
+PACK = 4
+WIDTH = 512
+J = 256
+Z = 1024
+HALF = J // 2
+LIST_COLS = J // 16
+FLOPS = 3 * 2 * 512 * 512 * J
+
+
+def tile_list_sum_picked_gated_plain_timeslook_pl_kernel(
+    tc, xt_words, xt_scales, w_words, w_scales, xo, fl, so, w2_words, w2_scales,
+    wb_words, wb_scales, tz, offs, offs2, offs3, out_0, out_1, out_2,
+):
+    nc = tc.nc
+    with ExitStack() as ctx:
+        sb = ctx.enter_context(tc.tile_pool(name="sb", bufs=1))
+        ps = ctx.enter_context(tc.psum_pool(name="ps", bufs=1))
+
+        def tile(name, shape, dtype):
+            return sb.tile(shape, dtype, name=name, align_bytes=64)
+
+        def words_ap(words):
+            return words[0].rearrange("p c r -> p (c r)").bitcast(I32)
+
+        def load_scales(engine, plane, scales):
+            for q in range(4):
+                engine.dma_start(
+                    out=plane[32 * q : 32 * q + 4, :].bitcast(I32),
+                    in_=scales[0, 4 * q : 4 * q + 4, :].bitcast(I32),
+                )
+
+        def deal(copy, dealt, raw):
+            copy(out=dealt.rearrange("p (t m) -> p m t", t=PACK), in_=raw.rearrange("p (m t) -> p m t", t=PACK))
+
+        def half_of(lst, h):
+            return lst[:, h * (LIST_COLS // 2) : (h + 1) * (LIST_COLS // 2)]
+
+        def interleave(copy, grouped, planes):
+            copy(
+                out=grouped.rearrange("p (c i t) -> p c t i", i=4, t=PACK),
+                in_=planes.rearrange("p t (c i) -> p c t i", i=4),
+            )
+
+        xt_sc = tile("xt_sc", [P, WIDTH], U8)
+        w_sc_raw = tile("w_sc_raw", [P, WIDTH], U8)
+        w2_sc_raw = tile("w2_sc_raw", [P, WIDTH], U8)
+        wb_sc_raw = tile("wb_sc_raw", [P, WIDTH], U8)
+        nc.vector.memset(xt_sc[:].bitcast(I32), 0)
+        nc.vector.memset(w_sc_raw[:].bitcast(I32), 0)
+        nc.gpsimd.memset(w2_sc_raw[:].bitcast(I32), 0)
+        nc.vector.memset(wb_sc_raw[:].bitcast(I32), 0)
+
+        list1 = sb.tile([P, LIST_COLS], U16, name="list1")
+        list2 = sb.tile([P, LIST_COLS], U16, name="list2")
+        list3 = sb.tile([P, LIST_COLS], U16, name="list3")
+        so_sb = tile("so_sb", [P, PACK, J], F32)
+        fl_sb = tile("fl_sb", [P, PACK], F32)
+        xt_w = tile("xt_w", [P, WIDTH], U32)
+        w_raw = tile("w_raw", [P, WIDTH], U32)
+        w2_raw = tile("w2_raw", [P, WIDTH], U32)
+        wb_raw = tile("wb_raw", [P, 2 * WIDTH], U8)
+        xo_pl = [tile("xo%d" % t, [P, Z], F32) for t in range(PACK)]
+        tz_pair = [tile("tz%d" % u, [P, 2, WIDTH], F32) for u in range(2)]
+
+        xo_rows = xo.rearrange("(p t) z -> p t z", t=PACK)
+        tz_rows = tz.rearrange("(p t) c -> p t c", t=PACK)
+        nc.sync.dma_start(list1[:], offs)
+        nc.scalar.dma_start(out=fl_sb[:], in_=fl.rearrange("(p t) o -> p (t o)", t=PACK))
+        load_scales(nc.scalar, xt_sc, xt_scales)
+        load_scales(nc.gpsimd, w2_sc_raw, w2_scales)
+        nc.sync.dma_start(out=so_sb[:], in_=so.rearrange("(p t) j -> p t j", t=PACK))
+        nc.sync.dma_start(out=xt_w[:].bitcast(I32), in_=words_ap(xt_words))
+        nc.sync.dma_start(out=w_raw[:].bitcast(I32), in_=words_ap(w_words))
+        nc.sync.dma_start(list2[:], offs2)
+        load_scales(nc.sync, w_sc_raw, w_scales)
+        for t in range(PACK):
+            nc.sync.dma_start(out=xo_pl[t][:], in_=xo_rows[:, t, :])
+        nc.sync.dma_start(out=w2_raw[:].bitcast(I32), in_=words_ap(w2_words))
+        nc.sync.dma_start(list3[:], offs3)
+        nc.sync.dma_start(out=wb_raw[:].bitcast(I32), in_=wb_words[0].bitcast(I32))
+        nc.sync.dma_start(out=tz_pair[0][:], in_=tz_rows[:, 0:2, :])
+        load_scales(nc.sync, wb_sc_raw, wb_scales)
+        nc.sync.dma_start(out=tz_pair[1][:], in_=tz_rows[:, 2:4, :])
+
+        sig = tile("sig", [P, PACK, J], F32)
+        gate = tile("gate", [P, PACK, J], F32)
+        for t in range(PACK):
+            nc.scalar.activation(out=sig[:, t, :], in_=so_sb[:, t, :], func=ACT.Sigmoid)
+            nc.scalar.activation(out=gate[:, t, :], in_=sig[:, t, :], func=ACT.Copy, scale=fl_sb[:, t : t + 1])
+        xt_g = tile("xt_g", [P, J], U32)
+        xt_g_sc = tile("xt_g_sc", [P, J], U8)
+        nc.vector.tensor_copy(out=xt_g[:], in_=xt_w[:].indirect(list1[:]))
+        nc.vector.tensor_copy(out=xt_g_sc[:], in_=xt_sc[:].indirect(list1[:]))
+        w_d = tile("w_d", [P, WIDTH], U32)
+        w_sc = tile("w_sc", [P, WIDTH], U8)
+        deal(nc.scalar.copy, w_d[:], w_raw[:])
+        deal(nc.vector.tensor_copy, w_sc[:], w_sc_raw[:])
+
+        acc1 = [ps.tile([P, PACK, HALF], F32, name="acc1_%d" % h) for h in range(2)]
+        acc2 = [ps.tile([P, PACK, HALF], F32, name="acc2_%d" % h) for h in range(2)]
+        for h in range(2):
+            cols = slice(h * HALF, (h + 1) * HALF)
+            for t in range(PACK):
+                m = slice(t * P, (t + 1) * P)
+                nc.tensor.matmul_mx(
+                    out=acc1[h][:, t, :], lhsT=w_d[:, m].bitcast(E4M3), lhsT_scale=w_sc[:, m],
+                    rhs=xt_g[:, cols].bitcast(E5M2), rhs_scale=xt_g_sc[:, cols], start=(t == 0), stop=False,
+                )
+
+        w2_d = tile("w2_d", [P, WIDTH], U32)
+        w2_sc = tile("w2_sc", [P, WIDTH], U8)
+        deal(nc.gpsimd.tensor_copy, w2_sc[:], w2_sc_raw[:])
+
+        u2 = [tile("u2_%d" % h, [P, PACK, HALF], F32) for h in range(2)]
+        u2_bf = [tile("u2_bf%d" % h, [P, HALF * PACK], BF16) for h in range(2)]
+        u2_q = [tile("u2_q%d" % h, [P, HALF], U32) for h in range(2)]
+        u2_sc = [tile("u2_sc%d" % h, [P, HALF], U8) for h in range(2)]
+
+        def pick_xo(t, h):
+            nc.vector.tensor_tensor(
+                out=u2[h][:, t, :], in0=xo_pl[t][:].indirect(half_of(list2, h)),
+                in1=gate[:, t, h * HALF : (h + 1) * HALF], op=ALU.mult,
+            )
+
+        for t in range(PACK - 1):
+            for h in range(2):
+                pick_xo(t, h)
+        pick_xo(PACK - 1, 0)
+        interleave(nc.vector.tensor_copy, u2_bf[0][:], u2[0][:])
+        pick_xo(PACK - 1, 1)
+        deal(nc.scalar.copy, w2_d[:], w2_raw[:])
+        nc.vector.quantize_mx(out=u2_q[0][:].bitcast(E4M3), scales=u2_sc[0][:], in_=u2_bf[0][:])
+        interleave(nc.vector.tensor_copy, u2_bf[1][:], u2[1][:])
+        wb_d = tile("wb_d", [P, 2 * WIDTH], U8)
+        wb_sc = tile("wb_sc", [P, WIDTH], U8)
+        deal(nc.scalar.copy, wb_d[:].bitcast(U16), wb_raw[:].bitcast(U16))
+        nc.vector.quantize_mx(out=u2_q[1][:].bitcast(E4M3), scales=u2_sc[1][:], in_=u2_bf[1][:])
+        deal(nc.vector.tensor_copy, wb_sc[:], wb_sc_raw[:])
+
+        for h in range(2):
+            for t in range(PACK):
+                m = slice(t * P, (t + 1) * P)
+                nc.tensor.matmul_mx(
+                    out=acc1[h][:, t, :], lhsT=w2_d[:, m].bitcast(E5M2), lhsT_scale=w2_sc[:, m],
+                    rhs=u2_q[h][:].bitcast(E4M3), rhs_scale=u2_sc[h][:], start=False, stop=(t == PACK - 1),
+                )
+
+        tz_g = [tile("tz_g%d" % h, [P, PACK, HALF], F32) for h in range(2)]
+
+        def pick_tz(t, h):
+            picked = tz_pair[t // 2][:, t % 2, :].indirect(half_of(list3, h))
+            if h == 0:
+                nc.vector.tensor_copy(out=tz_g[h][:, t, :], in_=picked)
+            else:
+                nc.scalar.activation(out=tz_g[h][:, t, :], in_=picked, func=ACT.Copy)
+
+        hid_bf = [tile("hid_bf%d" % h, [P, HALF * PACK], BF16) for h in range(2)]
+        hid_q = [tile("hid_q%d" % h, [P, HALF], U32) for h in range(2)]
+        hid_sc = [tile("hid_sc%d" % h, [P, HALF], U8) for h in range(2)]
+        for h in range(2):
+            nc.scalar.activation(
+                out=hid_bf[h][:].rearrange("p (j t) -> p j t", t=PACK),
+                in_=acc1[h][:].rearrange("p t j -> p j t"), func=ACT.Relu,
+            )
+            nc.vector.quantize_mx(out=hid_q[h][:].bitcast(E5M2), scales=hid_sc[h][:], in_=hid_bf[h][:])
+        for h in range(2):
+            for t in range(PACK):
+                pick_tz(t, h)
+        for h in range(2):
+            for t in range(PACK):
+                nc.tensor.matmul_mx(
+                    out=acc2[h][:, t, :], lhsT=wb_d[:, 2 * t * P : 2 * (t + 1) * P].bitcast(E2M1),
+                    lhsT_scale=wb_sc[:, t * P : (t + 1) * P],
+                    rhs=hid_q[h][:].bitcast(E5M2), rhs_scale=hid_sc[h][:], start=True, stop=True,
+                )
+
+        y = [tile("y%d" % h, [P, PACK, HALF], F32) for h in range(2)]
+        y_bf = [tile("y_bf%d" % h, [P, HALF * PACK], BF16) for h in range(2)]
+        y_q = tile("y_q", [P, J], U32)
+        y_sc = tile("y_sc", [P, J], U8)
+        out_rows = out_0.rearrange("(p t) j -> p t j", t=PACK)
+        for h in range(2):
+            nc.vector.tensor_tensor(out=y[h][:], in0=acc2[h][:], in1=tz_g[h][:], op=ALU.mult)
+            nc.sync.dma_start(out=out_rows[:, :, h * HALF : (h + 1) * HALF], in_=y[h][:])
+        interleave(nc.scalar.copy, y_bf[0][:], y[0][:])
+        interleave(nc.vector.tensor_copy, y_bf[1][:], y[1][:])
+        for h in range(2):
+            cols = slice(h * HALF, (h + 1) * HALF)
+            nc.vector.quantize_mx(out=y_q[:, cols].bitcast(E4M3), scales=y_sc[:, cols], in_=y_bf[h][:])
+        nc.sync.dma_start(out=words_ap(out_1), in_=y_q[:].bitcast(I32))
+        for q in range(4):
+            engine = nc.scalar if q % 2 == 0 else nc.sync
+            engine.dma_start(out=out_2[0, 4 * q : 4 * q + 4, :].bitcast(I32), in_=y_sc[32 * q : 32 * q + 4, :].bitcast(I32))

@@ -39,13 +39,6 @@ def tile_list_sum_picked_gated_plain_timeslook_pl_kernel(
         def words_ap(words):
             return words[0].rearrange("p c r -> p (c r)").bitcast(I32)
 
-        def load_scales(engine, plane, scales):
-            for q in range(4):
-                engine.dma_start(
-                    out=plane[32 * q : 32 * q + 4, :].bitcast(I32),
-                    in_=scales[0, 4 * q : 4 * q + 4, :].bitcast(I32),
-                )
-
         def deal(copy, dealt, raw):
             copy(out=dealt.rearrange("p (t m) -> p m t", t=PACK), in_=raw.rearrange("p (m t) -> p m t", t=PACK))
 
@@ -59,13 +52,14 @@ def tile_list_sum_picked_gated_plain_timeslook_pl_kernel(
             )
 
         xt_sc = tile("xt_sc", [P, WIDTH], U8)
-        w_sc_raw = tile("w_sc_raw", [P, WIDTH], U8)
-        w2_sc_raw = tile("w2_sc_raw", [P, WIDTH], U8)
-        wb_sc_raw = tile("wb_sc_raw", [P, WIDTH], U8)
+        sc_rows = tile("sc_rows", [16, 3 * WIDTH], U8)
+        sc_all = tile("sc_all", [P, 3 * WIDTH], U8)
+        xt_sc_rows = tile("xt_sc_rows", [P, WIDTH // 4], I32)
         nc.vector.memset(xt_sc[:].bitcast(I32), 0)
-        nc.vector.memset(w_sc_raw[:].bitcast(I32), 0)
-        nc.gpsimd.memset(w2_sc_raw[:].bitcast(I32), 0)
-        nc.vector.memset(wb_sc_raw[:].bitcast(I32), 0)
+        nc.vector.memset(sc_all[:].bitcast(I32), 0)
+        w_sc_raw = sc_all[:, 0:WIDTH]
+        w2_sc_raw = sc_all[:, WIDTH : 2 * WIDTH]
+        wb_sc_raw = sc_all[:, 2 * WIDTH : 3 * WIDTH]
 
         list1 = sb.tile([P, LIST_COLS], U16, name="list1")
         list2 = sb.tile([P, LIST_COLS], U16, name="list2")
@@ -77,41 +71,76 @@ def tile_list_sum_picked_gated_plain_timeslook_pl_kernel(
         w2_raw = tile("w2_raw", [P, WIDTH], U32)
         wb_raw = tile("wb_raw", [P, 2 * WIDTH], U8)
         xo_pl = [tile("xo%d" % t, [P, Z], F32) for t in range(PACK)]
-        tz_pair = [tile("tz%d" % u, [P, 2, WIDTH], F32) for u in range(2)]
+        tz_pl = [sb.tile([P, WIDTH], F32, name="tz%d" % t, tag="tz%d" % t, align_bytes=64) for t in range(PACK)]
 
         xo_rows = xo.rearrange("(p t) z -> p t z", t=PACK)
         tz_rows = tz.rearrange("(p t) c -> p t c", t=PACK)
+        for i, scales in enumerate((w_scales, w2_scales, wb_scales)):
+            engine = nc.scalar if i == 1 else nc.sync
+            engine.dma_start(out=sc_rows[:, i * WIDTH : (i + 1) * WIDTH].bitcast(I32), in_=scales[0].bitcast(I32))
+        for q, engine in enumerate((nc.scalar, nc.scalar, nc.gpsimd, nc.gpsimd)):
+            engine.dma_start(out=xt_sc_rows[32 * q : 32 * q + 4, :], in_=xt_scales[0, 4 * q : 4 * q + 4, :].bitcast(I32))
+        nc.gpsimd.dma_start(out=fl_sb[:], in_=fl.rearrange("(p t) o -> p (t o)", t=PACK))
         nc.sync.dma_start(list1[:], offs)
-        nc.scalar.dma_start(out=fl_sb[:], in_=fl.rearrange("(p t) o -> p (t o)", t=PACK))
-        load_scales(nc.scalar, xt_sc, xt_scales)
-        load_scales(nc.gpsimd, w2_sc_raw, w2_scales)
-        nc.sync.dma_start(out=so_sb[:], in_=so.rearrange("(p t) j -> p t j", t=PACK))
         nc.sync.dma_start(out=xt_w[:].bitcast(I32), in_=words_ap(xt_words))
-        nc.sync.dma_start(out=w_raw[:].bitcast(I32), in_=words_ap(w_words))
+        nc.sync.dma_start(out=so_sb[:], in_=so.rearrange("(p t) j -> p t j", t=PACK))
+        nc.sync.dma_start(out=xo_pl[0][:], in_=xo_rows[:, 0, :])
         nc.sync.dma_start(list2[:], offs2)
-        load_scales(nc.sync, w_sc_raw, w_scales)
-        for t in range(PACK):
-            nc.sync.dma_start(out=xo_pl[t][:], in_=xo_rows[:, t, :])
+        for q in range(4):
+            nc.sync.dma_start(out=sc_all[32 * q : 32 * q + 4, :].bitcast(I32), in_=sc_rows[4 * q : 4 * q + 4, :].bitcast(I32))
+        nc.sync.dma_start(out=xo_pl[1][:], in_=xo_rows[:, 1, :])
+        nc.sync.dma_start(out=w_raw[:].bitcast(I32), in_=words_ap(w_words))
+        nc.sync.dma_start(out=xo_pl[2][:], in_=xo_rows[:, 2, :])
+        nc.sync.dma_start(out=wb_raw[:].bitcast(I32), in_=wb_words[0].bitcast(I32))
+        nc.sync.dma_start(out=xo_pl[3][:], in_=xo_rows[:, 3, :])
         nc.sync.dma_start(out=w2_raw[:].bitcast(I32), in_=words_ap(w2_words))
         nc.sync.dma_start(list3[:], offs3)
-        nc.sync.dma_start(out=wb_raw[:].bitcast(I32), in_=wb_words[0].bitcast(I32))
-        nc.sync.dma_start(out=tz_pair[0][:], in_=tz_rows[:, 0:2, :])
-        load_scales(nc.sync, wb_sc_raw, wb_scales)
-        nc.sync.dma_start(out=tz_pair[1][:], in_=tz_rows[:, 2:4, :])
+        for t in range(PACK):
+            nc.sync.dma_start(out=tz_pl[t][:], in_=tz_rows[:, t, :])
 
         sig = tile("sig", [P, PACK, J], F32)
-        gate = tile("gate", [P, PACK, J], F32)
+        gate = tile("gate", [P, HALF], F32)
+        last = PACK - 1
         for t in range(PACK):
             nc.scalar.activation(out=sig[:, t, :], in_=so_sb[:, t, :], func=ACT.Sigmoid)
-            nc.scalar.activation(out=gate[:, t, :], in_=sig[:, t, :], func=ACT.Copy, scale=fl_sb[:, t : t + 1])
+        nc.scalar.activation(out=gate[:], in_=sig[:, last, 0:HALF], func=ACT.Copy, scale=fl_sb[:, last : last + 1])
         xt_g = tile("xt_g", [P, J], U32)
         xt_g_sc = tile("xt_g_sc", [P, J], U8)
+        for q in range(4):
+            nc.vector.tensor_copy(out=xt_sc[32 * q : 32 * q + 4, :].bitcast(I32), in_=xt_sc_rows[32 * q : 32 * q + 4, :])
         nc.vector.tensor_copy(out=xt_g[:], in_=xt_w[:].indirect(list1[:]))
         nc.vector.tensor_copy(out=xt_g_sc[:], in_=xt_sc[:].indirect(list1[:]))
-        w_d = tile("w_d", [P, WIDTH], U32)
         w_sc = tile("w_sc", [P, WIDTH], U8)
+        deal(nc.vector.tensor_copy, w_sc[:], w_sc_raw)
+        w2_d = tile("w2_d", [P, WIDTH], U32)
+        w2_sc = tile("w2_sc", [P, WIDTH], U8)
+        deal(nc.vector.tensor_copy, w2_sc[:], w2_sc_raw)
+        wb_d = tile("wb_d", [P, 2 * WIDTH], U8)
+        wb_sc = tile("wb_sc", [P, WIDTH], U8)
+        deal(nc.vector.tensor_copy, wb_sc[:], wb_sc_raw)
+
+        u2 = tile("u2", [P, 2, PACK, HALF], F32)
+        u2_bf = [tile("u2_bf%d" % h, [P, HALF * PACK], BF16) for h in range(2)]
+        u2_q = [tile("u2_q%d" % h, [P, HALF], U32) for h in range(2)]
+        u2_sc = [tile("u2_sc%d" % h, [P, HALF], U8) for h in range(2)]
+
+        def gate_plane(t, picked):
+            nc.vector.scalar_tensor_tensor(
+                out=u2[:, :, t, :], in0=sig[:, t, :].rearrange("p (h j) -> p h j", h=2), scalar=fl_sb[:, t : t + 1],
+                in1=picked.rearrange("p (h j) -> p h j", h=2), op0=ALU.mult, op1=ALU.mult,
+            )
+
+        xo_g = [tile("xo_g%d" % t, [P, J], F32) for t in range(last)]
+        xo_g3 = tile("xo_g3", [P, HALF], F32)
+
+        def pick_plane(t):
+            nc.scalar.activation(out=xo_g[t][:], in_=xo_pl[t][:].indirect(list2[:]), func=ACT.Copy)
+            gate_plane(t, xo_g[t][:])
+
+        pick_plane(0)
+        pick_plane(1)
+        w_d = tile("w_d", [P, WIDTH], U32)
         deal(nc.scalar.copy, w_d[:], w_raw[:])
-        deal(nc.vector.tensor_copy, w_sc[:], w_sc_raw[:])
 
         acc1 = [ps.tile([P, PACK, HALF], F32, name="acc1_%d" % h) for h in range(2)]
         acc2 = [ps.tile([P, PACK, HALF], F32, name="acc2_%d" % h) for h in range(2)]
@@ -124,35 +153,21 @@ def tile_list_sum_picked_gated_plain_timeslook_pl_kernel(
                     rhs=xt_g[:, cols].bitcast(E5M2), rhs_scale=xt_g_sc[:, cols], start=(t == 0), stop=False,
                 )
 
-        w2_d = tile("w2_d", [P, WIDTH], U32)
-        w2_sc = tile("w2_sc", [P, WIDTH], U8)
-        deal(nc.gpsimd.tensor_copy, w2_sc[:], w2_sc_raw[:])
-
-        u2 = [tile("u2_%d" % h, [P, PACK, HALF], F32) for h in range(2)]
-        u2_bf = [tile("u2_bf%d" % h, [P, HALF * PACK], BF16) for h in range(2)]
-        u2_q = [tile("u2_q%d" % h, [P, HALF], U32) for h in range(2)]
-        u2_sc = [tile("u2_sc%d" % h, [P, HALF], U8) for h in range(2)]
-
-        def pick_xo(t, h):
-            nc.vector.tensor_tensor(
-                out=u2[h][:, t, :], in0=xo_pl[t][:].indirect(half_of(list2, h)),
-                in1=gate[:, t, h * HALF : (h + 1) * HALF], op=ALU.mult,
-            )
-
-        for t in range(PACK - 1):
-            for h in range(2):
-                pick_xo(t, h)
-        pick_xo(PACK - 1, 0)
-        interleave(nc.vector.tensor_copy, u2_bf[0][:], u2[0][:])
-        pick_xo(PACK - 1, 1)
+        pick_plane(2)
+        deal(nc.scalar.copy, wb_d[:].bitcast(U16), wb_raw[:].bitcast(U16))
+        nc.vector.tensor_tensor(
+            out=u2[:, 0, last, :], in0=xo_pl[last][:].indirect(half_of(list2, 0)), in1=gate[:], op=ALU.mult,
+        )
+        nc.scalar.activation(out=xo_g3[:], in_=xo_pl[last][:].indirect(half_of(list2, 1)), func=ACT.Copy)
+        interleave(nc.vector.tensor_copy, u2_bf[0][:], u2[:, 0, :, :])
+        nc.vector.scalar_tensor_tensor(
+            out=u2[:, 1, last, :], in0=sig[:, last, HALF:J], scalar=fl_sb[:, last : last + 1],
+            in1=xo_g3[:], op0=ALU.mult, op1=ALU.mult,
+        )
         deal(nc.scalar.copy, w2_d[:], w2_raw[:])
         nc.vector.quantize_mx(out=u2_q[0][:].bitcast(E4M3), scales=u2_sc[0][:], in_=u2_bf[0][:])
-        interleave(nc.vector.tensor_copy, u2_bf[1][:], u2[1][:])
-        wb_d = tile("wb_d", [P, 2 * WIDTH], U8)
-        wb_sc = tile("wb_sc", [P, WIDTH], U8)
-        deal(nc.scalar.copy, wb_d[:].bitcast(U16), wb_raw[:].bitcast(U16))
+        interleave(nc.vector.tensor_copy, u2_bf[1][:], u2[:, 1, :, :])
         nc.vector.quantize_mx(out=u2_q[1][:].bitcast(E4M3), scales=u2_sc[1][:], in_=u2_bf[1][:])
-        deal(nc.vector.tensor_copy, wb_sc[:], wb_sc_raw[:])
 
         for h in range(2):
             for t in range(PACK):
@@ -162,33 +177,26 @@ def tile_list_sum_picked_gated_plain_timeslook_pl_kernel(
                     rhs=u2_q[h][:].bitcast(E4M3), rhs_scale=u2_sc[h][:], start=False, stop=(t == PACK - 1),
                 )
 
-        tz_g = [tile("tz_g%d" % h, [P, PACK, HALF], F32) for h in range(2)]
-
-        def pick_tz(t, h):
-            picked = tz_pair[t // 2][:, t % 2, :].indirect(half_of(list3, h))
-            if h == 0:
-                nc.vector.tensor_copy(out=tz_g[h][:, t, :], in_=picked)
-            else:
-                nc.scalar.activation(out=tz_g[h][:, t, :], in_=picked, func=ACT.Copy)
-
-        hid_bf = [tile("hid_bf%d" % h, [P, HALF * PACK], BF16) for h in range(2)]
-        hid_q = [tile("hid_q%d" % h, [P, HALF], U32) for h in range(2)]
+        tz_g = tile("tz_g", [P, PACK, J], F32)
+        for t in range(2):
+            nc.scalar.activation(out=tz_g[:, t, :], in_=tz_pl[t][:].indirect(list3[:]), func=ACT.Copy)
+        for t in (2, 3):
+            nc.vector.tensor_copy(out=tz_g[:, t, :], in_=tz_pl[t][:].indirect(list3[:]))
+        hid_bf = sb.tile([P, 2, HALF * PACK], BF16, name="hid_bf", tag="tz1", align_bytes=64)
+        hid_q = sb.tile([P, 2, HALF], U32, name="hid_q", tag="tz3", align_bytes=64)
         hid_sc = [tile("hid_sc%d" % h, [P, HALF], U8) for h in range(2)]
         for h in range(2):
             nc.scalar.activation(
-                out=hid_bf[h][:].rearrange("p (j t) -> p j t", t=PACK),
+                out=hid_bf[:, h, :].rearrange("p (j t) -> p j t", t=PACK),
                 in_=acc1[h][:].rearrange("p t j -> p j t"), func=ACT.Relu,
             )
-            nc.vector.quantize_mx(out=hid_q[h][:].bitcast(E5M2), scales=hid_sc[h][:], in_=hid_bf[h][:])
-        for h in range(2):
-            for t in range(PACK):
-                pick_tz(t, h)
+            nc.vector.quantize_mx(out=hid_q[:, h, :].bitcast(E5M2), scales=hid_sc[h][:], in_=hid_bf[:, h, :])
         for h in range(2):
             for t in range(PACK):
                 nc.tensor.matmul_mx(
                     out=acc2[h][:, t, :], lhsT=wb_d[:, 2 * t * P : 2 * (t + 1) * P].bitcast(E2M1),
                     lhsT_scale=wb_sc[:, t * P : (t + 1) * P],
-                    rhs=hid_q[h][:].bitcast(E5M2), rhs_scale=hid_sc[h][:], start=True, stop=True,
+                    rhs=hid_q[:, h, :].bitcast(E5M2), rhs_scale=hid_sc[h][:], start=True, stop=True,
                 )
 
         y = [tile("y%d" % h, [P, PACK, HALF], F32) for h in range(2)]
@@ -197,14 +205,14 @@ def tile_list_sum_picked_gated_plain_timeslook_pl_kernel(
         y_sc = tile("y_sc", [P, J], U8)
         out_rows = out_0.rearrange("(p t) j -> p t j", t=PACK)
         for h in range(2):
-            nc.vector.tensor_tensor(out=y[h][:], in0=acc2[h][:], in1=tz_g[h][:], op=ALU.mult)
+            nc.vector.tensor_tensor(out=y[h][:], in0=acc2[h][:], in1=tz_g[:, :, h * HALF : (h + 1) * HALF], op=ALU.mult)
             nc.sync.dma_start(out=out_rows[:, :, h * HALF : (h + 1) * HALF], in_=y[h][:])
         interleave(nc.scalar.copy, y_bf[0][:], y[0][:])
         interleave(nc.vector.tensor_copy, y_bf[1][:], y[1][:])
         for h in range(2):
             cols = slice(h * HALF, (h + 1) * HALF)
             nc.vector.quantize_mx(out=y_q[:, cols].bitcast(E4M3), scales=y_sc[:, cols], in_=y_bf[h][:])
-        nc.sync.dma_start(out=words_ap(out_1), in_=y_q[:].bitcast(I32))
+            nc.sync.dma_start(out=words_ap(out_1)[:, cols], in_=y_q[:, cols].bitcast(I32))
         for q in range(4):
-            engine = nc.scalar if q % 2 == 0 else nc.sync
+            engine = nc.sync if q == 3 else nc.scalar
             engine.dma_start(out=out_2[0, 4 * q : 4 * q + 4, :].bitcast(I32), in_=y_sc[32 * q : 32 * q + 4, :].bitcast(I32))

@@ -101,9 +101,7 @@ def tile_list_sum_picked_gated_plain_timeslook_pl_kernel(
         sig = tile("sig", [P, PACK, J], F32)
         gate = tile("gate", [P, HALF], F32)
         last = PACK - 1
-        for t in range(PACK):
-            nc.scalar.activation(out=sig[:, t, :], in_=so_sb[:, t, :], func=ACT.Sigmoid)
-        nc.scalar.activation(out=gate[:], in_=sig[:, last, 0:HALF], func=ACT.Copy, scale=fl_sb[:, last : last + 1])
+        nc.scalar.activation(out=sig[:], in_=so_sb[:], func=ACT.Sigmoid)
         xt_g = tile("xt_g", [P, J], U32)
         xt_g_sc = tile("xt_g_sc", [P, J], U8)
         for q in range(4):
@@ -139,6 +137,9 @@ def tile_list_sum_picked_gated_plain_timeslook_pl_kernel(
 
         pick_plane(0)
         pick_plane(1)
+        nc.vector.tensor_scalar(
+            out=gate[:], in0=sig[:, last, 0:HALF], scalar1=fl_sb[:, last : last + 1], scalar2=None, op0=ALU.mult
+        )
         w_d = tile("w_d", [P, WIDTH], U32)
         deal(nc.scalar.copy, w_d[:], w_raw[:])
 
@@ -180,10 +181,9 @@ def tile_list_sum_picked_gated_plain_timeslook_pl_kernel(
         tz_g = tile("tz_g", [P, PACK, J], F32)
         for t in range(2):
             nc.scalar.activation(out=tz_g[:, t, :], in_=tz_pl[t][:].indirect(list3[:]), func=ACT.Copy)
-        for t in (2, 3):
-            nc.vector.tensor_copy(out=tz_g[:, t, :], in_=tz_pl[t][:].indirect(list3[:]))
+        nc.vector.tensor_copy(out=tz_g[:, 2, :], in_=tz_pl[2][:].indirect(list3[:]))
         hid_bf = sb.tile([P, 2, HALF * PACK], BF16, name="hid_bf", tag="tz1", align_bytes=64)
-        hid_q = sb.tile([P, 2, HALF], U32, name="hid_q", tag="tz3", align_bytes=64)
+        hid_q = sb.tile([P, 2, HALF], U32, name="hid_q", tag="tz2", align_bytes=64)
         hid_sc = [tile("hid_sc%d" % h, [P, HALF], U8) for h in range(2)]
         for h in range(2):
             nc.scalar.activation(
@@ -191,6 +191,8 @@ def tile_list_sum_picked_gated_plain_timeslook_pl_kernel(
                 in_=acc1[h][:].rearrange("p t j -> p j t"), func=ACT.Relu,
             )
             nc.vector.quantize_mx(out=hid_q[:, h, :].bitcast(E5M2), scales=hid_sc[h][:], in_=hid_bf[:, h, :])
+        nc.vector.tensor_copy(out=tz_g[:, last, 0:HALF], in_=tz_pl[last][:].indirect(half_of(list3, 0)))
+        nc.scalar.activation(out=tz_g[:, last, HALF:J], in_=tz_pl[last][:].indirect(half_of(list3, 1)), func=ACT.Copy)
         for h in range(2):
             for t in range(PACK):
                 nc.tensor.matmul_mx(
@@ -212,7 +214,7 @@ def tile_list_sum_picked_gated_plain_timeslook_pl_kernel(
         for h in range(2):
             cols = slice(h * HALF, (h + 1) * HALF)
             nc.vector.quantize_mx(out=y_q[:, cols].bitcast(E4M3), scales=y_sc[:, cols], in_=y_bf[h][:])
-            nc.sync.dma_start(out=words_ap(out_1)[:, cols], in_=y_q[:, cols].bitcast(I32))
+            nc.scalar.dma_start(out=words_ap(out_1)[:, cols], in_=y_q[:, cols].bitcast(I32))
         for q in range(4):
-            engine = nc.sync if q == 3 else nc.scalar
+            engine = nc.sync if q >= 2 else nc.scalar
             engine.dma_start(out=out_2[0, 4 * q : 4 * q + 4, :].bitcast(I32), in_=y_sc[32 * q : 32 * q + 4, :].bitcast(I32))

from contextlib import ExitStack

import concourse.mybir as mybir

F32 = mybir.dt.float32
BF16 = mybir.dt.bfloat16
I32 = mybir.dt.int32
U32 = mybir.dt.uint32
U16 = mybir.dt.uint16
U8 = mybir.dt.uint8
E4M3 = mybir.dt.float8_e4m3fn_x4
E5M2 = mybir.dt.float8_e5m2_x4
E2M1 = mybir.dt.float4_e2m1fn_x4
ACT = mybir.ActivationFunctionType
ALU = mybir.AluOpType

P = 128
PACK = 4
WIDTH = 512
J = 256
Z = 1024
HALF = J // 2
LIST_COLS = J // 16
FLOPS = 3 * 2 * 512 * 512 * J


def tile_list_sum_picked_gated_plain_timeslook_pl_kernel(
    tc, xt_words, xt_scales, w_words, w_scales, xo, fl, so, w2_words, w2_scales,
    wb_words, wb_scales, tz, offs, offs2, offs3, out_0, out_1, out_2,
):
    nc = tc.nc
    with ExitStack() as ctx:
        sb = ctx.enter_context(tc.tile_pool(name="sb", bufs=1))
        ps = ctx.enter_context(tc.psum_pool(name="ps", bufs=1))

        def tile(name, shape, dtype):
            return sb.tile(shape, dtype, name=name, align_bytes=64)

        def words_ap(words):
            return words[0].rearrange("p c r -> p (c r)").bitcast(I32)

        def deal(copy, dealt, raw):
            copy(out=dealt.rearrange("p (t m) -> p m t", t=PACK), in_=raw.rearrange("p (m t) -> p m t", t=PACK))

        def half_of(lst, h):
            return lst[:, h * (LIST_COLS // 2) : (h + 1) * (LIST_COLS // 2)]

        def interleave(copy, grouped, planes):
            copy(
                out=grouped.rearrange("p (c i t) -> p c t i", i=4, t=PACK),
                in_=planes.rearrange("p t (c i) -> p c t i", i=4),
            )

        xt_sc = tile("xt_sc", [P, WIDTH], U8)
        sc_rows = tile("sc_rows", [16, 3 * WIDTH], U8)
        sc_all = tile("sc_all", [P, 3 * WIDTH], U8)
        xt_sc_rows = tile("xt_sc_rows", [P, WIDTH // 4], I32)
        nc.vector.memset(xt_sc[:].bitcast(I32), 0)
        nc.vector.memset(sc_all[:].bitcast(I32), 0)
        w_sc_raw = sc_all[:, 0:WIDTH]
        w2_sc_raw = sc_all[:, WIDTH : 2 * WIDTH]
        wb_sc_raw = sc_all[:, 2 * WIDTH : 3 * WIDTH]

        list1 = sb.tile([P, LIST_COLS], U16, name="list1")
        list2 = sb.tile([P, LIST_COLS], U16, name="list2")
        list3 = sb.tile([P, LIST_COLS], U16, name="list3")
        so_sb = tile("so_sb", [P, PACK, J], F32)
        fl_sb = tile("fl_sb", [P, PACK], F32)
        xt_w = tile("xt_w", [P, WIDTH], U32)
        w_raw = tile("w_raw", [P, WIDTH], U32)
        w2_raw = tile("w2_raw", [P, WIDTH], U32)
        wb_raw = tile("wb_raw", [P, 2 * WIDTH], U8)
        xo_pl = [tile("xo%d" % t, [P, Z], F32) for t in range(PACK)]
        tz_pl = [sb.tile([P, WIDTH], F32, name="tz%d" % t, tag="tz%d" % t, align_bytes=64) for t in range(PACK)]

        xo_rows = xo.rearrange("(p t) z -> p t z", t=PACK)
        tz_rows = tz.rearrange("(p t) c -> p t c", t=PACK)
        for i, scales in enumerate((w_scales, w2_scales, wb_scales)):
            engine = nc.scalar if i == 1 else nc.sync
            engine.dma_start(out=sc_rows[:, i * WIDTH : (i + 1) * WIDTH].bitcast(I32), in_=scales[0].bitcast(I32))
        for q, engine in enumerate((nc.scalar, nc.scalar, nc.gpsimd, nc.gpsimd)):
            engine.dma_start(out=xt_sc_rows[32 * q : 32 * q + 4, :], in_=xt_scales[0, 4 * q : 4 * q + 4, :].bitcast(I32))
        nc.gpsimd.dma_start(out=fl_sb[:], in_=fl.rearrange("(p t) o -> p (t o)", t=PACK))
        nc.sync.dma_start(list1[:], offs)
        nc.sync.dma_start(out=xt_w[:].bitcast(I32), in_=words_ap(xt_words))
        nc.sync.dma_start(out=so_sb[:], in_=so.rearrange("(p t) j -> p t j", t=PACK))
        nc.sync.dma_start(out=xo_pl[0][:], in_=xo_rows[:, 0, :])
        nc.sync.dma_start(list2[:], offs2)
        for q in range(4):
            nc.sync.dma_start(out=sc_all[32 * q : 32 * q + 4, :].bitcast(I32), in_=sc_rows[4 * q : 4 * q + 4, :].bitcast(I32))
        nc.sync.dma_start(out=xo_pl[1][:], in_=xo_rows[:, 1, :])
        nc.sync.dma_start(out=w_raw[:].bitcast(I32), in_=words_ap(w_words))
        nc.sync.dma_start(out=xo_pl[2][:], in_=xo_rows[:, 2, :])
        nc.sync.dma_start(out=wb_raw[:].bitcast(I32), in_=wb_words[0].bitcast(I32))
        nc.sync.dma_start(out=xo_pl[3][:], in_=xo_rows[:, 3, :])
        nc.sync.dma_start(out=w2_raw[:].bitcast(I32), in_=words_ap(w2_words))
        nc.sync.dma_start(list3[:], offs3)
        for t in range(PACK):
            nc.sync.dma_start(out=tz_pl[t][:], in_=tz_rows[:, t, :])

        sig = tile("sig", [P, PACK, J], F32)
        gate = tile("gate", [P, HALF], F32)
        last = PACK - 1
        nc.scalar.activation(out=sig[:], in_=so_sb[:], func=ACT.Sigmoid)
        xt_g = tile("xt_g", [P, J], U32)
        xt_g_sc = tile("xt_g_sc", [P, J], U8)
        for q in range(4):
            nc.vector.tensor_copy(out=xt_sc[32 * q : 32 * q + 4, :].bitcast(I32), in_=xt_sc_rows[32 * q : 32 * q + 4, :])
        nc.vector.tensor_copy(out=xt_g[:], in_=xt_w[:].indirect(list1[:]))
        nc.vector.tensor_copy(out=xt_g_sc[:], in_=xt_sc[:].indirect(list1[:]))
        w_sc = tile("w_sc", [P, WIDTH], U8)
        deal(nc.vector.tensor_copy, w_sc[:], w_sc_raw)
        w2_d = tile("w2_d", [P, WIDTH], U32)
        w2_sc = tile("w2_sc", [P, WIDTH], U8)
        deal(nc.vector.tensor_copy, w2_sc[:], w2_sc_raw)
        wb_d = tile("wb_d", [P, 2 * WIDTH], U8)
        wb_sc = tile("wb_sc", [P, WIDTH], U8)
        deal(nc.vector.tensor_copy, wb_sc[:], wb_sc_raw)

        u2 = tile("u2", [P, 2, PACK, HALF], F32)
        u2_bf = [tile("u2_bf%d" % h, [P, HALF * PACK], BF16) for h in range(2)]
        u2_q = [tile("u2_q%d" % h, [P, HALF], U32) for h in range(2)]
        u2_sc = [tile("u2_sc%d" % h, [P, HALF], U8) for h in range(2)]

        def gate_plane(t, picked):
            nc.vector.scalar_tensor_tensor(
                out=u2[:, :, t, :], in0=sig[:, t, :].rearrange("p (h j) -> p h j", h=2), scalar=fl_sb[:, t : t + 1],
                in1=picked.rearrange("p (h j) -> p h j", h=2), op0=ALU.mult, op1=ALU.mult,
            )

        xo_g = [tile("xo_g%d" % t, [P, J], F32) for t in range(last)]
        xo_g3 = tile("xo_g3", [P, HALF], F32)

        def pick_plane(t):
            nc.scalar.activation(out=xo_g[t][:], in_=xo_pl[t][:].indirect(list2[:]), func=ACT.Copy)
            gate_plane(t, xo_g[t][:])

        pick_plane(0)
        pick_plane(1)
        nc.vector.tensor_scalar(
            out=gate[:], in0=sig[:, last, 0:HALF], scalar1=fl_sb[:, last : last + 1], scalar2=None, op0=ALU.mult
        )
        w_d = tile("w_d", [P, WIDTH], U32)
        deal(nc.scalar.copy, w_d[:], w_raw[:])

        acc1 = [ps.tile([P, PACK, HALF], F32, name="acc1_%d" % h) for h in range(2)]
        acc2 = [ps.tile([P, PACK, HALF], F32, name="acc2_%d" % h) for h in range(2)]
        for h in range(2):
            cols = slice(h * HALF, (h + 1) * HALF)
            for t in range(PACK):
                m = slice(t * P, (t + 1) * P)
                nc.tensor.matmul_mx(
                    out=acc1[h][:, t, :], lhsT=w_d[:, m].bitcast(E4M3), lhsT_scale=w_sc[:, m],
                    rhs=xt_g[:, cols].bitcast(E5M2), rhs_scale=xt_g_sc[:, cols], start=(t == 0), stop=False,
                )

        pick_plane(2)
        deal(nc.scalar.copy, wb_d[:].bitcast(U16), wb_raw[:].bitcast(U16))
        nc.vector.tensor_tensor(
            out=u2[:, 0, last, :], in0=xo_pl[last][:].indirect(half_of(list2, 0)), in1=gate[:], op=ALU.mult,
        )
        nc.scalar.activation(out=xo_g3[:], in_=xo_pl[last][:].indirect(half_of(list2, 1)), func=ACT.Copy)
        interleave(nc.vector.tensor_copy, u2_bf[0][:], u2[:, 0, :, :])
        nc.vector.scalar_tensor_tensor(
            out=u2[:, 1, last, :], in0=sig[:, last, HALF:J], scalar=fl_sb[:, last : last + 1],
            in1=xo_g3[:], op0=ALU.mult, op1=ALU.mult,
        )
        deal(nc.scalar.copy, w2_d[:], w2_raw[:])
        nc.vector.quantize_mx(out=u2_q[0][:].bitcast(E4M3), scales=u2_sc[0][:], in_=u2_bf[0][:])
        interleave(nc.vector.tensor_copy, u2_bf[1][:], u2[:, 1, :, :])
        nc.vector.quantize_mx(out=u2_q[1][:].bitcast(E4M3), scales=u2_sc[1][:], in_=u2_bf[1][:])

        for h in range(2):
            for t in range(PACK):
                m = slice(t * P, (t + 1) * P)
                nc.tensor.matmul_mx(
                    out=acc1[h][:, t, :], lhsT=w2_d[:, m].bitcast(E5M2), lhsT_scale=w2_sc[:, m],
                    rhs=u2_q[h][:].bitcast(E4M3), rhs_scale=u2_sc[h][:], start=False, stop=(t == PACK - 1),
                )

        tz_g = tile("tz_g", [P, PACK, J], F32)
        for t in range(2):
            nc.scalar.activation(out=tz_g[:, t, :], in_=tz_pl[t][:].indirect(list3[:]), func=ACT.Copy)
        nc.vector.tensor_copy(out=tz_g[:, 2, :], in_=tz_pl[2][:].indirect(list3[:]))
        hid_bf = sb.tile([P, 2, HALF * PACK], BF16, name="hid_bf", tag="tz1", align_bytes=64)
        hid_q = sb.tile([P, 2, HALF], U32, name="hid_q", tag="tz2", align_bytes=64)
        hid_sc = [tile("hid_sc%d" % h, [P, HALF], U8) for h in range(2)]
        for h in range(2):
            nc.scalar.activation(
                out=hid_bf[:, h, :].rearrange("p (j t) -> p j t", t=PACK),
                in_=acc1[h][:].rearrange("p t j -> p j t"), func=ACT.Relu,
            )
            nc.vector.quantize_mx(out=hid_q[:, h, :].bitcast(E5M2), scales=hid_sc[h][:], in_=hid_bf[:, h, :])
        nc.vector.tensor_copy(out=tz_g[:, last, 0:HALF], in_=tz_pl[last][:].indirect(half_of(list3, 0)))
        nc.scalar.activation(out=tz_g[:, last, HALF:J], in_=tz_pl[last][:].indirect(half_of(list3, 1)), func=ACT.Copy)
        for h in range(2):
            for t in range(PACK):
                nc.tensor.matmul_mx(
                    out=acc2[h][:, t, :], lhsT=wb_d[:, 2 * t * P : 2 * (t + 1) * P].bitcast(E2M1),
                    lhsT_scale=wb_sc[:, t * P : (t + 1) * P],
                    rhs=hid_q[:, h, :].bitcast(E5M2), rhs_scale=hid_sc[h][:], start=True, stop=True,
                )

        y = [tile("y%d" % h, [P, PACK, HALF], F32) for h in range(2)]
        y_bf = [tile("y_bf%d" % h, [P, HALF * PACK], BF16) for h in range(2)]
        y_q = tile("y_q", [P, J], U32)
        y_sc = tile("y_sc", [P, J], U8)
        out_rows = out_0.rearrange("(p t) j -> p t j", t=PACK)
        for h in range(2):
            nc.vector.tensor_tensor(out=y[h][:], in0=acc2[h][:], in1=tz_g[:, :, h * HALF : (h + 1) * HALF], op=ALU.mult)
            nc.sync.dma_start(out=out_rows[:, :, h * HALF : (h + 1) * HALF], in_=y[h][:])
        interleave(nc.scalar.copy, y_bf[0][:], y[0][:])
        interleave(nc.vector.tensor_copy, y_bf[1][:], y[1][:])
        for h in range(2):
            cols = slice(h * HALF, (h + 1) * HALF)
            nc.vector.quantize_mx(out=y_q[:, cols].bitcast(E4M3), scales=y_sc[:, cols], in_=y_bf[h][:])
            nc.scalar.dma_start(out=words_ap(out_1)[:, cols], in_=y_q[:, cols].bitcast(I32))
        for q in range(4):
            engine = nc.sync if q >= 2 else nc.scalar
            engine.dma_start(out=out_2[0, 4 * q : 4 * q + 4, :].bitcast(I32), in_=y_sc[32 * q : 32 * q + 4, :].bitcast(I32))
